import numpy as np
import ml_dtypes

BF16 = ml_dtypes.bfloat16


def bf(x):
    return np.asarray(x, np.float32).astype(BF16)


def f32(x):
    return np.asarray(x, np.float32)


def f64(x):
    return np.asarray(x).astype(np.float64)


def striped(idx):
    return np.tile(idx.reshape(-1, 16).T, (8, 1))


S, K, M, N = 1024, 256, 256, 128


def setup_inputs():
    return {"table": bf(np.random.standard_normal((S, K))), "w": bf(np.random.standard_normal((K, M)) / np.sqrt(K)), "s": f32(0.5 + np.random.random_sample((M, 1))), "b": f32(0.5 * np.random.standard_normal((M, 1))), "offs": striped(np.sort(np.random.permutation(S)[:N]))}


def reference(table, w, s, b, offs):
    idx = offs[:16].T.reshape(-1)
    x = f64(table)[idx].T
    y = f64(w).T @ x
    return y * f64(s) + f64(b)

@@ -1,0 +1,87 @@
+import concourse.mybir as mybir
+from concourse.masks import make_identity
+
+BF16 = mybir.dt.bfloat16
+F32 = mybir.dt.float32
+U16 = mybir.dt.uint16
+
+P = 128
+S, K, M, N = 1024, 256, 256, 128
+TOKEN_BLOCKS = S // P
+K_BLOCKS = K // P
+M_BLOCKS = M // P
+PAIR = 2
+WARMING = 16
+
+FLOPS = 2 * K * M * N
+
+
+def tile_gather_matmul_kernel(tc, table, w, s, b, offs, out):
+    nc = tc.nc
+    with (
+        tc.tile_pool(name="held", bufs=1) as held,
+        tc.psum_pool(name="flipped", bufs=5) as flipped,
+        tc.psum_pool(name="sums", bufs=1) as sums,
+    ):
+        rows = []
+        for g in range(TOKEN_BLOCKS // PAIR):
+            pair = held.tile([P, PAIR, K], BF16, name="rows%d" % g)
+            nc.sync.dma_start(
+                pair[:], table[g * PAIR * P : (g + 1) * PAIR * P, :].rearrange("(i p) k -> p i k", p=P)
+            )
+            rows.append(pair)
+        weights = held.tile([P, K_BLOCKS, M], BF16, name="weights")
+        nc.sync.dma_start(weights[:], w.rearrange("(kb p) m -> p kb m", p=P))
+        offsets = held.tile([P, N // 16], U16, name="offsets")
+        nc.sync.dma_start(offsets[:], offs)
+        gain = held.tile([P, M_BLOCKS], F32, name="gain")
+        shift = held.tile([P, M_BLOCKS], F32, name="shift")
+        with nc.allow_non_contiguous_dma(reason="one float32 to a partition for each block of output features"):
+            nc.sync.dma_start(gain[:], s.rearrange("(mb p) o -> p (mb o)", p=P))
+            nc.sync.dma_start(shift[:], b.rearrange("(mb p) o -> p (mb o)", p=P))
+
+        zeros = held.tile([P, P], BF16, name="zeros")
+        nc.gpsimd.memset(zeros[:], 0.0)
+        unread = sums.tile([P, P], F32, name="unread")
+        for n in range(WARMING):
+            nc.tensor.matmul(unread[:], zeros[:], zeros[:], start=True, stop=True)
+
+        identity = held.tile([P, P], BF16, name="identity")
+        make_identity(nc, identity[:])
+
+        windows = [held.tile([P, S], BF16, name="window%d" % kb) for kb in range(K_BLOCKS)]
+        for g in range(TOKEN_BLOCKS // PAIR):
+            turned = [flipped.tile([P, PAIR * P], BF16, name="turned") for kb in range(K_BLOCKS)]
+            for kb in range(K_BLOCKS):
+                for i in range(PAIR):
+                    nc.tensor.transpose(
+                        turned[kb][:, i * P : (i + 1) * P],
+                        rows[g][:, i, kb * P : (kb + 1) * P],
+                        identity[:],
+                    )
+            for kb in range(K_BLOCKS):
+                nc.vector.tensor_copy(windows[kb][:, g * PAIR * P : (g + 1) * PAIR * P], turned[kb][:])
+
+        y = [sums.tile([P, N], F32, name="y%d" % mb) for mb in range(M_BLOCKS)]
+        for kb in range(K_BLOCKS):
+            for mb in range(M_BLOCKS):
+                nc.tensor.matmul(
+                    y[mb][:],
+                    weights[:, kb, mb * P : (mb + 1) * P],
+                    windows[kb][:].indirect(offsets[:]),
+                    start=(kb == 0),
+                    stop=(kb == K_BLOCKS - 1),
+                )
+
+        for mb in range(M_BLOCKS):
+            result = held.tile([P, N], F32, name="result%d" % mb)
+            nc.vector.tensor_scalar(
+                result[:],
+                y[mb][:],
+                gain[:, mb : mb + 1],
+                shift[:, mb : mb + 1],
+                op0=mybir.AluOpType.mult,
+                op1=mybir.AluOpType.add,
+            )
+            queue = nc.sync if mb % 2 == 0 else nc.scalar
+            queue.dma_start(out[mb * P : (mb + 1) * P, :], result[:])

@@ -83,5 +83,4 @@ def tile_gather_matmul_kernel(tc, table, w, s, b, offs, out):
                 op0=mybir.AluOpType.mult,
                 op1=mybir.AluOpType.add,
             )
-            queue = nc.sync if mb % 2 == 0 else nc.scalar
-            queue.dma_start(out[mb * P : (mb + 1) * P, :], result[:])
+            nc.sync.dma_start(out[mb * P : (mb + 1) * P, :], result[:])

@@ -40,11 +40,12 @@ def tile_gather_matmul_kernel(tc, table, w, s, b, offs, out):
             nc.sync.dma_start(gain[:], s.rearrange("(mb p) o -> p (mb o)", p=P))
             nc.sync.dma_start(shift[:], b.rearrange("(mb p) o -> p (mb o)", p=P))
 
-        zeros = held.tile([P, P], BF16, name="zeros")
+        zeros = held.tile([P, 2], BF16, name="zeros")
         nc.gpsimd.memset(zeros[:], 0.0)
+        repeated = zeros[:, 0:1].to_broadcast([P, P])
         unread = sums.tile([P, P], F32, name="unread")
         for n in range(WARMING):
-            nc.tensor.matmul(unread[:], zeros[:], zeros[:], start=True, stop=True)
+            nc.tensor.matmul(unread[:], repeated, repeated, start=True, stop=True)
 
         identity = held.tile([P, P], BF16, name="identity")
         make_identity(nc, identity[:])

@@ -10,7 +10,8 @@ S, K, M, N = 1024, 256, 256, 128
 TOKEN_BLOCKS = S // P
 K_BLOCKS = K // P
 M_BLOCKS = M // P
-PAIR = 2
+CHUNKS = (3, 3, 2)
+assert sum(CHUNKS) == TOKEN_BLOCKS
 WARMING = 16
 
 FLOPS = 2 * K * M * N
@@ -24,12 +25,14 @@ def tile_gather_matmul_kernel(tc, table, w, s, b, offs, out):
         tc.psum_pool(name="sums", bufs=1) as sums,
     ):
         rows = []
-        for g in range(TOKEN_BLOCKS // PAIR):
-            pair = held.tile([P, PAIR, K], BF16, name="rows%d" % g)
+        starts = [sum(CHUNKS[:g]) for g in range(len(CHUNKS))]
+        for g, blocks in enumerate(CHUNKS):
+            chunk = held.tile([P, blocks, K], BF16, name="rows%d" % g)
             nc.sync.dma_start(
-                pair[:], table[g * PAIR * P : (g + 1) * PAIR * P, :].rearrange("(i p) k -> p i k", p=P)
+                chunk[:],
+                table[starts[g] * P : (starts[g] + blocks) * P, :].rearrange("(i p) k -> p i k", p=P),
             )
-            rows.append(pair)
+            rows.append(chunk)
         weights = held.tile([P, K_BLOCKS, M], BF16, name="weights")
         nc.sync.dma_start(weights[:], w.rearrange("(kb p) m -> p kb m", p=P))
         offsets = held.tile([P, N // 16], U16, name="offsets")
@@ -51,17 +54,17 @@ def tile_gather_matmul_kernel(tc, table, w, s, b, offs, out):
         make_identity(nc, identity[:])
 
         windows = [held.tile([P, S], BF16, name="window%d" % kb) for kb in range(K_BLOCKS)]
-        for g in range(TOKEN_BLOCKS // PAIR):
-            turned = [flipped.tile([P, PAIR * P], BF16, name="turned") for kb in range(K_BLOCKS)]
+        for g, blocks in enumerate(CHUNKS):
+            turned = [flipped.tile([P, blocks * P], BF16, name="turned") for kb in range(K_BLOCKS)]
             for kb in range(K_BLOCKS):
-                for i in range(PAIR):
+                for i in range(blocks):
                     nc.tensor.transpose(
                         turned[kb][:, i * P : (i + 1) * P],
                         rows[g][:, i, kb * P : (kb + 1) * P],
                         identity[:],
                     )
             for kb in range(K_BLOCKS):
-                nc.vector.tensor_copy(windows[kb][:, g * PAIR * P : (g + 1) * PAIR * P], turned[kb][:])
+                nc.vector.tensor_copy(windows[kb][:, starts[g] * P : (starts[g] + blocks) * P], turned[kb][:])
 
         y = [sums.tile([P, N], F32, name="y%d" % mb) for mb in range(M_BLOCKS)]
         for kb in range(K_BLOCKS):
@@ -74,14 +77,14 @@ def tile_gather_matmul_kernel(tc, table, w, s, b, offs, out):
                     stop=(kb == K_BLOCKS - 1),
                 )
 
+        result = held.tile([P, M_BLOCKS, N], F32, name="result")
         for mb in range(M_BLOCKS):
-            result = held.tile([P, N], F32, name="result%d" % mb)
             nc.vector.tensor_scalar(
-                result[:],
+                result[:, mb, :],
                 y[mb][:],
                 gain[:, mb : mb + 1],
                 shift[:, mb : mb + 1],
                 op0=mybir.AluOpType.mult,
                 op1=mybir.AluOpType.add,
             )
-            nc.sync.dma_start(out[mb * P : (mb + 1) * P, :], result[:])
+        nc.sync.dma_start(out.rearrange("(mb p) j -> p mb j", p=P), result[:])

@@ -10,7 +10,7 @@ S, K, M, N = 1024, 256, 256, 128
 TOKEN_BLOCKS = S // P
 K_BLOCKS = K // P
 M_BLOCKS = M // P
-CHUNKS = (3, 3, 2)
+CHUNKS = (2, 3, 3)
 assert sum(CHUNKS) == TOKEN_BLOCKS
 WARMING = 16
 

@@ -13,6 +13,7 @@ M_BLOCKS = M // P
 CHUNKS = (2, 3, 3)
 assert sum(CHUNKS) == TOKEN_BLOCKS
 WARMING = 16
+HOLDING = (0, 1, 2)
 
 FLOPS = 2 * K * M * N
 
@@ -46,9 +47,9 @@ def tile_gather_matmul_kernel(tc, table, w, s, b, offs, out):
         zeros = held.tile([P, 2], BF16, name="zeros")
         nc.gpsimd.memset(zeros[:], 0.0)
         repeated = zeros[:, 0:1].to_broadcast([P, P])
-        unread = sums.tile([P, P], F32, name="unread")
+        unread = sums.tile([P, K], F32, name="unread")
         for n in range(WARMING):
-            nc.tensor.matmul(unread[:], repeated, repeated, start=True, stop=True)
+            nc.tensor.matmul(unread[:, 0:P], repeated, repeated, start=True, stop=True)
 
         identity = held.tile([P, P], BF16, name="identity")
         make_identity(nc, identity[:])
@@ -63,6 +64,8 @@ def tile_gather_matmul_kernel(tc, table, w, s, b, offs, out):
                         rows[g][:, i, kb * P : (kb + 1) * P],
                         identity[:],
                     )
+            for n in range(HOLDING[g]):
+                nc.tensor.matmul(unread[:], identity[:], rows[g][:, 0, :], start=True, stop=True)
             for kb in range(K_BLOCKS):
                 nc.vector.tensor_copy(windows[kb][:, starts[g] * P : (starts[g] + blocks) * P], turned[kb][:])
 

import concourse.mybir as mybir
from concourse.masks import make_identity

BF16 = mybir.dt.bfloat16
F32 = mybir.dt.float32
U16 = mybir.dt.uint16

P = 128
S, K, M, N = 1024, 256, 256, 128
TOKEN_BLOCKS = S // P
K_BLOCKS = K // P
M_BLOCKS = M // P
CHUNKS = (2, 3, 3)
assert sum(CHUNKS) == TOKEN_BLOCKS
WARMING = 16
HOLDING = (0, 1, 2)

FLOPS = 2 * K * M * N


def tile_gather_matmul_kernel(tc, table, w, s, b, offs, out):
    nc = tc.nc
    with (
        tc.tile_pool(name="held", bufs=1) as held,
        tc.psum_pool(name="flipped", bufs=5) as flipped,
        tc.psum_pool(name="sums", bufs=1) as sums,
    ):
        rows = []
        starts = [sum(CHUNKS[:g]) for g in range(len(CHUNKS))]
        for g, blocks in enumerate(CHUNKS):
            chunk = held.tile([P, blocks, K], BF16, name="rows%d" % g)
            nc.sync.dma_start(
                chunk[:],
                table[starts[g] * P : (starts[g] + blocks) * P, :].rearrange("(i p) k -> p i k", p=P),
            )
            rows.append(chunk)
        weights = held.tile([P, K_BLOCKS, M], BF16, name="weights")
        nc.sync.dma_start(weights[:], w.rearrange("(kb p) m -> p kb m", p=P))
        offsets = held.tile([P, N // 16], U16, name="offsets")
        nc.sync.dma_start(offsets[:], offs)
        gain = held.tile([P, M_BLOCKS], F32, name="gain")
        shift = held.tile([P, M_BLOCKS], F32, name="shift")
        with nc.allow_non_contiguous_dma(reason="one float32 to a partition for each block of output features"):
            nc.sync.dma_start(gain[:], s.rearrange("(mb p) o -> p (mb o)", p=P))
            nc.sync.dma_start(shift[:], b.rearrange("(mb p) o -> p (mb o)", p=P))

        zeros = held.tile([P, 2], BF16, name="zeros")
        nc.gpsimd.memset(zeros[:], 0.0)
        repeated = zeros[:, 0:1].to_broadcast([P, P])
        unread = sums.tile([P, K], F32, name="unread")
        for n in range(WARMING):
            nc.tensor.matmul(unread[:, 0:P], repeated, repeated, start=True, stop=True)

        identity = held.tile([P, P], BF16, name="identity")
        make_identity(nc, identity[:])

        windows = [held.tile([P, S], BF16, name="window%d" % kb) for kb in range(K_BLOCKS)]
        for g, blocks in enumerate(CHUNKS):
            turned = [flipped.tile([P, blocks * P], BF16, name="turned") for kb in range(K_BLOCKS)]
            for kb in range(K_BLOCKS):
                for i in range(blocks):
                    nc.tensor.transpose(
                        turned[kb][:, i * P : (i + 1) * P],
                        rows[g][:, i, kb * P : (kb + 1) * P],
                        identity[:],
                    )
            for n in range(HOLDING[g]):
                nc.tensor.matmul(unread[:], identity[:], rows[g][:, 0, :], start=True, stop=True)
            for kb in range(K_BLOCKS):
                nc.vector.tensor_copy(windows[kb][:, starts[g] * P : (starts[g] + blocks) * P], turned[kb][:])

        y = [sums.tile([P, N], F32, name="y%d" % mb) for mb in range(M_BLOCKS)]
        for kb in range(K_BLOCKS):
            for mb in range(M_BLOCKS):
                nc.tensor.matmul(
                    y[mb][:],
                    weights[:, kb, mb * P : (mb + 1) * P],
                    windows[kb][:].indirect(offsets[:]),
                    start=(kb == 0),
                    stop=(kb == K_BLOCKS - 1),
                )

        result = held.tile([P, M_BLOCKS, N], F32, name="result")
        for mb in range(M_BLOCKS):
            nc.vector.tensor_scalar(
                result[:, mb, :],
                y[mb][:],
                gain[:, mb : mb + 1],
                shift[:, mb : mb + 1],
                op0=mybir.AluOpType.mult,
                op1=mybir.AluOpType.add,
            )
        nc.sync.dma_start(out.rearrange("(mb p) j -> p mb j", p=P), result[:])
